import numpy as np
import ml_dtypes


def mxq(x, axis, fmt="e4m3"):
    dtype, down = {"e4m3": (ml_dtypes.float8_e4m3fn, 7), "e5m2": (ml_dtypes.float8_e5m2, 14)}[fmt]
    v = np.moveaxis(np.asarray(x, np.float32).astype(ml_dtypes.bfloat16).astype(np.float64), axis, -1)
    blocks = v.reshape(v.shape[:-1] + (-1, 32))
    amax = np.abs(blocks).max(-1, keepdims=True)
    byte = np.maximum(np.where(amax > 0, np.frexp(amax)[1] - 1 + 127, 0) - down, 1)
    scale = np.exp2(byte - 127.0)
    codes = (blocks / scale).astype(np.float32).astype(dtype).astype(np.float64)
    return np.moveaxis((codes * scale).reshape(v.shape), -1, axis)


WIDE = False


def mx_kscale(k, group=512):
    if not WIDE:
        return np.ones(k)
    levels = np.array([10, -10, 5, -5, 0])
    if group != 512:
        return np.exp2(np.random.permutation(np.resize(levels, k // group))).repeat(group)
    if k % 512:
        return np.exp2(np.random.permutation(np.resize(levels, k // 32))).repeat(32)
    a = np.empty((k // 512, 16))
    for p in range(k // 512):
        a[p, :8] = np.random.permutation(np.resize(levels, 8))
        for g in range(8):
            far = levels[np.abs(levels - a[p, g]) >= 10]
            a[p, g + 8] = far[np.random.randint(len(far))]
    return np.exp2(a.ravel()).repeat(32)


def f64(x):
    return np.asarray(x).astype(np.float64)


def hswish(v):
    return v * np.minimum(np.maximum(v + 3.0, 0.0), 6.0) / 6.0


G, D, M, N, L = 2, 256, 128, 512, 768


def setup_inputs():
    n = np.random.standard_normal
    s_d = mx_kscale(D, 0)
    return {
        "x": (n((G, D, L)) * s_d[:, None]).astype(np.float32),
        "w0": (n((G, D, M)) / np.sqrt(3 * D) / s_d[:, None]).astype(np.float32),
        "w1": (n((G, D, M)) / np.sqrt(3 * D) / s_d[:, None]).astype(np.float32),
        "w2": (n((G, D, M)) / np.sqrt(3 * D) / s_d[:, None]).astype(np.float32),
        "cs": (np.random.uniform(0.5, 2.0, (G, M, 1))).astype(np.float32),
        "cb": (0.5 * n((G, M, 1))).astype(np.float32),
    }


def reference(x, w0, w1, w2, cs, cb):
    w0q = mxq(f64(w0), 1, "e4m3")
    xq = mxq(f64(x), 1, "e4m3")
    w1q = mxq(f64(w1), 1, "e4m3")
    w2q = mxq(f64(w2), 1, "e4m3")
    z = (w0q.transpose(0, 2, 1) @ xq[..., :512]) + (w1q.transpose(0, 2, 1) @ xq[..., 128 : 640]) + (w2q.transpose(0, 2, 1) @ xq[..., 256 : 768])
    y = hswish(z * f64(cs) + f64(cb))
    return y

@@ -1,0 +1,194 @@
+import math
+from contextlib import ExitStack
+
+import concourse.mybir as mybir
+
+G, D, M, N, L = 2, 256, 128, 512, 768
+TAPS = 3
+FLOPS = 2 * G * TAPS * D * M * N
+
+F32 = mybir.dt.float32
+BF16 = mybir.dt.bfloat16
+U32 = mybir.dt.uint32
+U8 = mybir.dt.uint8
+FP8X4 = mybir.dt.float8_e4m3fn_x4
+ACT = mybir.ActivationFunctionType
+ALU = mybir.AluOpType
+
+P = 128
+PACK = 4
+ROWS = D // PACK
+BLK = 128
+INV_SQRT6 = 1.0 / math.sqrt(6.0)
+HALF = 3.0 * INV_SQRT6
+
+
+def tile_rows_conv_bnhs_kernel(tc, x, w0, w1, w2, cs, cb, out):
+    nc = tc.nc
+    with ExitStack() as ctx:
+        sb = ctx.enter_context(tc.tile_pool(name="sb", bufs=1))
+        ps = ctx.enter_context(tc.psum_pool(name="ps", bufs=1))
+        ctx.enter_context(tc.manual_schedule())
+
+        x_rows = x.rearrange("g (p j) l -> (g p) j l", j=PACK)
+        chunks = [(0, 384), (384, 640), (640, 768)]
+        x_raw = [sb.tile([P, PACK, b - a], F32, name="x_raw%d" % i, align_bytes=64) for i, (a, b) in enumerate(chunks)]
+        w_raw = [sb.tile([P, PACK, M], F32, name="w_raw%d" % t, align_bytes=64) for t in range(TAPS)]
+        x_bf = sb.tile([P, L, PACK], BF16, name="x_bf", align_bytes=64)
+        w_bf = sb.tile([P, TAPS * M, PACK], BF16, name="w_bf", align_bytes=64)
+        x_codes = sb.tile([P, L], U32, name="x_codes", align_bytes=64)
+        x_scales = sb.tile([P, L], U8, name="x_scales", align_bytes=64)
+        w_codes = sb.tile([P, TAPS * M], U32, name="w_codes", align_bytes=64)
+        w_scales = sb.tile([P, TAPS * M], U8, name="w_scales", align_bytes=64)
+        norm_rows = sb.tile([P, P], F32, name="norm_rows", align_bytes=64)
+        norm_scaled = sb.tile([P, P], F32, name="norm_scaled", align_bytes=64)
+        norm = sb.tile([P, P], F32, name="norm", align_bytes=64)
+        shifted = sb.tile([P, G], F32, name="shifted", align_bytes=64)
+        acc = [[ps.tile([M, BLK], F32, name="acc%d_%d" % (g, b)) for b in range(N // BLK)] for g in range(G)]
+        lin = sb.tile([P, N // BLK, G, BLK], F32, name="lin", align_bytes=64)
+        gate = sb.tile([P, N // BLK, G, BLK], F32, name="gate", align_bytes=64)
+        res_a = sb.tile([P, G, BLK], F32, name="res_a", align_bytes=64)
+        res_b = sb.tile([P, G, 2 * BLK], F32, name="res_b", align_bytes=64)
+        res_c = sb.tile([P, G, BLK], F32, name="res_c", align_bytes=64)
+
+        def load_x(i):
+            a, b = chunks[i]
+            nc.sync.dma_start(out=x_raw[i][:], in_=x_rows[:, :, a:b])
+
+        def load_w(t, w):
+            nc.sync.dma_start(out=w_raw[t][:], in_=w.rearrange("g (p j) m -> (g p) j m", j=PACK))
+
+        def cast(copy, dst, src):
+            copy(out=dst.rearrange("p (c i) j -> p c j i", i=4), in_=src.rearrange("p j (c i) -> p c j i", i=4))
+
+        def cast_x(copy, a, b):
+            i = [k for k, (lo, hi) in enumerate(chunks) if lo <= a and b <= hi][0]
+            cast(copy, x_bf[:, a:b, :], x_raw[i][:, :, a - chunks[i][0] : b - chunks[i][0]])
+
+        def cast_w(copy, t):
+            cast(copy, w_bf[:, t * M : (t + 1) * M, :], w_raw[t][:])
+
+        def quantise(codes, scales, bf, a, b):
+            nc.vector.quantize_mx(
+                out=codes[:, a:b].bitcast(FP8X4), scales=scales[:, a:b], in_=bf[:, a:b, :].rearrange("p c j -> p (c j)")
+            )
+
+        def multiply(b, t):
+            for g in range(G):
+                rows = slice(ROWS * g, ROWS * (g + 1))
+                wc = slice(t * M, (t + 1) * M)
+                xc = slice((b + t) * BLK, (b + t + 1) * BLK)
+                nc.tensor.matmul_mx(
+                    out=acc[g][b][:],
+                    lhsT=w_codes[rows, wc].bitcast(FP8X4),
+                    lhsT_scale=w_scales[rows, wc],
+                    rhs=x_codes[rows, xc].bitcast(FP8X4),
+                    rhs_scale=x_scales[rows, xc],
+                    start=(t == 0),
+                    stop=(t == TAPS - 1),
+                )
+
+        def factor(g):
+            return norm[:, 32 * g : 32 * g + 1]
+
+        def shift(g):
+            return norm[:, 64 + 32 * g : 64 + 32 * g + 1]
+
+        def lin_scalar(b, g):
+            nc.scalar.activation(out=lin[:, b, g, :], in_=acc[g][b][:], func=ACT.Identity, scale=factor(g), bias=shift(g))
+
+        def lin_vector(b, g):
+            nc.vector.tensor_scalar(
+                out=lin[:, b, g, :], in0=acc[g][b][:], scalar1=factor(g), scalar2=shift(g), op0=ALU.mult, op1=ALU.add
+            )
+
+        def gate_scalar(b, g):
+            nc.scalar.activation(
+                out=gate[:, b, g, :], in_=acc[g][b][:], func=ACT.Relu, scale=factor(g), bias=shifted[:, g : g + 1]
+            )
+
+        def finish_relu(dst, b, gs):
+            nc.vector.scalar_tensor_tensor(
+                out=dst, in0=gate[:, b, gs, :], scalar=2.0 * HALF, in1=lin[:, b, gs, :], op0=ALU.min, op1=ALU.mult
+            )
+
+        def clamp(b):
+            nc.vector.tensor_scalar(
+                out=gate[:, b, :, :], in0=lin[:, b, :, :], scalar1=-HALF, scalar2=HALF, op0=ALU.max, op1=ALU.min
+            )
+
+        def finish_clamp(dst, b):
+            nc.vector.scalar_tensor_tensor(
+                out=dst, in0=gate[:, b, :, :], scalar=HALF, in1=lin[:, b, :, :], op0=ALU.add, op1=ALU.mult
+            )
+
+        out_rows = out.rearrange("g m n -> m g n")
+        vcopy = nc.vector.tensor_copy
+        scopy = nc.scalar.copy
+
+        load_x(0)
+        load_w(0, w0)
+        load_w(1, w1)
+        load_w(2, w2)
+        load_x(1)
+        load_x(2)
+
+        nc.vector.memset(norm_rows[:], 0.0)
+        for k, v in enumerate((cs, cb)):
+            nc.scalar.dma_start(
+                out=norm_rows[0:P:32, 64 * k : 64 * (k + 1)].rearrange("q (g i) -> q g i", g=G),
+                in_=v.rearrange("g (q i) o -> q g (i o)", i=32),
+            )
+        nc.scalar.activation(out=norm_scaled[:], in_=norm_rows[:], func=ACT.Copy, scale=INV_SQRT6)
+        nc.vector.transpose(norm[:], norm_scaled[:])
+        nc.vector.tensor_scalar(out=shifted[:], in0=norm[:, 64:P:32], scalar1=HALF, scalar2=None, op0=ALU.add)
+
+        cast_x(vcopy, 0, 256)
+        cast_x(scopy, 256, 384)
+        cast_w(scopy, 0)
+        quantise(x_codes, x_scales, x_bf, 256, 384)
+        quantise(x_codes, x_scales, x_bf, 0, 256)
+        cast_w(vcopy, 1)
+        quantise(w_codes, w_scales, w_bf, 0, M)
+        cast_w(scopy, 2)
+        quantise(w_codes, w_scales, w_bf, M, 2 * M)
+        multiply(0, 0)
+        multiply(1, 0)
+        multiply(2, 0)
+        multiply(0, 1)
+        multiply(1, 1)
+        quantise(w_codes, w_scales, w_bf, 2 * M, 3 * M)
+        multiply(0, 2)
+        lin_scalar(0, 0)
+        lin_scalar(0, 1)
+        cast_x(vcopy, 384, 544)
+        cast_x(scopy, 544, 640)
+        clamp(0)
+        quantise(x_codes, x_scales, x_bf, 384, 640)
+        multiply(1, 2)
+        multiply(2, 1)
+        multiply(2, 2)
+        multiply(3, 0)
+        multiply(3, 1)
+        finish_clamp(res_a[:], 0)
+        nc.sync.dma_start(out=out_rows[:, :, 0:BLK], in_=res_a[:])
+        cast_x(scopy, 704, 768)
+        cast_x(vcopy, 640, 704)
+        lin_scalar(1, 0)
+        lin_scalar(1, 1)
+        lin_vector(2, 0)
+        quantise(x_codes, x_scales, x_bf, 640, 768)
+        multiply(3, 2)
+        lin_scalar(2, 1)
+        clamp(1)
+        clamp(2)
+        finish_clamp(res_b[:, :, 0:BLK], 1)
+        finish_clamp(res_b[:, :, BLK : 2 * BLK], 2)
+        nc.sync.dma_start(out=out_rows[:, :, BLK : 3 * BLK], in_=res_b[:])
+        gate_scalar(3, 0)
+        lin_scalar(3, 0)
+        gate_scalar(3, 1)
+        lin_vector(3, 1)
+        finish_relu(res_c[:, 0:1, :], 3, slice(0, 1))
+        finish_relu(res_c[:, 1:2, :], 3, slice(1, 2))
+        nc.sync.dma_start(out=out_rows[:, :, 3 * BLK : 4 * BLK], in_=res_c[:])

@@ -30,165 +30,208 @@ def tile_rows_conv_bnhs_kernel(tc, x, w0, w1, w2, cs, cb, out):
         ps = ctx.enter_context(tc.psum_pool(name="ps", bufs=1))
         ctx.enter_context(tc.manual_schedule())
 
-        x_rows = x.rearrange("g (p j) l -> (g p) j l", j=PACK)
-        chunks = [(0, 384), (384, 640), (640, 768)]
-        x_raw = [sb.tile([P, PACK, b - a], F32, name="x_raw%d" % i, align_bytes=64) for i, (a, b) in enumerate(chunks)]
-        w_raw = [sb.tile([P, PACK, M], F32, name="w_raw%d" % t, align_bytes=64) for t in range(TAPS)]
-        x_bf = sb.tile([P, L, PACK], BF16, name="x_bf", align_bytes=64)
-        w_bf = sb.tile([P, TAPS * M, PACK], BF16, name="w_bf", align_bytes=64)
-        x_codes = sb.tile([P, L], U32, name="x_codes", align_bytes=64)
-        x_scales = sb.tile([P, L], U8, name="x_scales", align_bytes=64)
-        w_codes = sb.tile([P, TAPS * M], U32, name="w_codes", align_bytes=64)
-        w_scales = sb.tile([P, TAPS * M], U8, name="w_scales", align_bytes=64)
+        src = {"x": x.rearrange("g (p j) l -> (g p) j l", j=PACK)}
+        w_src = [w.rearrange("g (p j) m -> (g p) j m", j=PACK) for w in (w0, w1, w2)]
+        width = {"x": L, "w": TAPS * M}
+        pieces = [("w", 0, 128), ("x", 0, 512), ("w", 128, 256), ("w", 256, 384), ("x", 512, 640), ("x", 640, 768)]
+        raw = {pc: sb.tile([P, PACK, pc[2] - pc[1]], F32, name="raw_%s%d" % pc[:2], align_bytes=64) for pc in pieces}
+        bf = {n: sb.tile([P, width[n], PACK], BF16, name="bf_" + n, align_bytes=64) for n in width}
+        codes = {n: sb.tile([P, width[n]], U32, name="codes_" + n, align_bytes=64) for n in width}
+        scales = {n: sb.tile([P, width[n]], U8, name="scales_" + n, align_bytes=64) for n in width}
         norm_rows = sb.tile([P, P], F32, name="norm_rows", align_bytes=64)
-        norm_scaled = sb.tile([P, P], F32, name="norm_scaled", align_bytes=64)
-        norm = sb.tile([P, P], F32, name="norm", align_bytes=64)
+        norm_cols = sb.tile([P, P], F32, name="norm_cols", align_bytes=64)
+        norm = sb.tile([P, 2 * G], F32, name="norm", align_bytes=64)
         shifted = sb.tile([P, G], F32, name="shifted", align_bytes=64)
-        acc = [[ps.tile([M, BLK], F32, name="acc%d_%d" % (g, b)) for b in range(N // BLK)] for g in range(G)]
+        one = sb.tile([P, 1], F32, name="one", align_bytes=64)
+        half = sb.tile([P, 1], F32, name="half", align_bytes=64)
+        acc = [[ps.tile([M, BLK], F32, name="acc%d_%d" % (g, b)) for b in range(N // BLK - g)] for g in range(G)]
+        acc[1].append(acc[1][0])
+        spare = ps.tile([M, BLK], F32, name="spare")
         lin = sb.tile([P, N // BLK, G, BLK], F32, name="lin", align_bytes=64)
         gate = sb.tile([P, N // BLK, G, BLK], F32, name="gate", align_bytes=64)
-        res_a = sb.tile([P, G, BLK], F32, name="res_a", align_bytes=64)
-        res_b = sb.tile([P, G, 2 * BLK], F32, name="res_b", align_bytes=64)
-        res_c = sb.tile([P, G, BLK], F32, name="res_c", align_bytes=64)
+        res = sb.tile([P, N // BLK, G, BLK], F32, name="res", align_bytes=64)
+        out_rows = out.rearrange("g m n -> m g n")
 
-        def load_x(i):
-            a, b = chunks[i]
-            nc.sync.dma_start(out=x_raw[i][:], in_=x_rows[:, :, a:b])
+        def load(n, a, b):
+            nc.sync.dma_start(out=raw[(n, a, b)][:], in_=src["x"][:, :, a:b] if n == "x" else w_src[a // M])
 
-        def load_w(t, w):
-            nc.sync.dma_start(out=w_raw[t][:], in_=w.rearrange("g (p j) m -> (g p) j m", j=PACK))
-
-        def cast(copy, dst, src):
-            copy(out=dst.rearrange("p (c i) j -> p c j i", i=4), in_=src.rearrange("p j (c i) -> p c j i", i=4))
-
-        def cast_x(copy, a, b):
-            i = [k for k, (lo, hi) in enumerate(chunks) if lo <= a and b <= hi][0]
-            cast(copy, x_bf[:, a:b, :], x_raw[i][:, :, a - chunks[i][0] : b - chunks[i][0]])
-
-        def cast_w(copy, t):
-            cast(copy, w_bf[:, t * M : (t + 1) * M, :], w_raw[t][:])
-
-        def quantise(codes, scales, bf, a, b):
-            nc.vector.quantize_mx(
-                out=codes[:, a:b].bitcast(FP8X4), scales=scales[:, a:b], in_=bf[:, a:b, :].rearrange("p c j -> p (c j)")
+        def load_norm(k):
+            nc.sync.dma_start(
+                out=norm_rows[0:P:32, 64 * k : 64 * (k + 1)].rearrange("q (g i) -> q g i", g=G),
+                in_=(cs, cb)[k].rearrange("g (q i) o -> q g (i o)", i=32),
             )
 
-        def multiply(b, t):
-            for g in range(G):
-                rows = slice(ROWS * g, ROWS * (g + 1))
-                wc = slice(t * M, (t + 1) * M)
-                xc = slice((b + t) * BLK, (b + t + 1) * BLK)
+        def cast(copy, n, a, b):
+            pc = [k for k in pieces if k[0] == n and k[1] <= a and b <= k[2]][0]
+            copy(
+                out=bf[n][:, a:b, :].rearrange("p (c i) j -> p c j i", i=4),
+                in_=raw[pc][:, :, a - pc[1] : b - pc[1]].rearrange("p j (c i) -> p c j i", i=4),
+            )
+
+        def quantise(n, a, b):
+            nc.vector.quantize_mx(
+                out=codes[n][:, a:b].bitcast(FP8X4),
+                scales=scales[n][:, a:b],
+                in_=bf[n][:, a:b, :].rearrange("p c j -> p (c j)"),
+            )
+
+        def pass_mx(dst, g, wc, xc, start, stop):
+            rows = slice(ROWS * g, ROWS * (g + 1))
+            nc.tensor.matmul_mx(
+                out=dst,
+                lhsT=codes["w"][rows, wc].bitcast(FP8X4),
+                lhsT_scale=scales["w"][rows, wc],
+                rhs=codes["x"][rows, xc].bitcast(FP8X4),
+                rhs_scale=scales["x"][rows, xc],
+                start=start,
+                stop=stop,
+            )
+
+        def multiply(b, t, g):
+            pass_mx(
+                acc[g][b][:, 0:BLK], g, slice(t * M, (t + 1) * M), slice((b + t) * BLK, (b + t + 1) * BLK),
+                t == 0, t == TAPS - 1,
+            )
+
+        def warm(n):
+            for i in range(n):
                 nc.tensor.matmul_mx(
-                    out=acc[g][b][:],
-                    lhsT=w_codes[rows, wc].bitcast(FP8X4),
-                    lhsT_scale=w_scales[rows, wc],
-                    rhs=x_codes[rows, xc].bitcast(FP8X4),
-                    rhs_scale=x_scales[rows, xc],
-                    start=(t == 0),
-                    stop=(t == TAPS - 1),
+                    out=spare[:],
+                    lhsT=codes["w"][:, 0:M].bitcast(FP8X4),
+                    lhsT_scale=scales["w"][:, 0:M],
+                    rhs=codes["w"][:, 0:M].bitcast(FP8X4),
+                    rhs_scale=scales["w"][:, 0:M],
+                    start=True,
+                    stop=True,
                 )
 
-        def factor(g):
-            return norm[:, 32 * g : 32 * g + 1]
-
-        def shift(g):
-            return norm[:, 64 + 32 * g : 64 + 32 * g + 1]
-
         def lin_scalar(b, g):
-            nc.scalar.activation(out=lin[:, b, g, :], in_=acc[g][b][:], func=ACT.Identity, scale=factor(g), bias=shift(g))
+            nc.scalar.activation(
+                out=lin[:, b, g, :], in_=acc[g][b][:, 0:BLK], func=ACT.Identity,
+                scale=norm[:, g : g + 1], bias=norm[:, G + g : G + g + 1],
+            )
 
         def lin_vector(b, g):
             nc.vector.tensor_scalar(
-                out=lin[:, b, g, :], in0=acc[g][b][:], scalar1=factor(g), scalar2=shift(g), op0=ALU.mult, op1=ALU.add
+                out=lin[:, b, g, :], in0=acc[g][b][:, 0:BLK], scalar1=norm[:, g : g + 1],
+                scalar2=norm[:, G + g : G + g + 1], op0=ALU.mult, op1=ALU.add,
             )
 
         def gate_scalar(b, g):
             nc.scalar.activation(
-                out=gate[:, b, g, :], in_=acc[g][b][:], func=ACT.Relu, scale=factor(g), bias=shifted[:, g : g + 1]
+                out=gate[:, b, g, :], in_=acc[g][b][:, 0:BLK], func=ACT.Relu,
+                scale=norm[:, g : g + 1], bias=shifted[:, g : g + 1],
             )
 
-        def finish_relu(dst, b, gs):
+        def finish_relu(b, gs):
             nc.vector.scalar_tensor_tensor(
-                out=dst, in0=gate[:, b, gs, :], scalar=2.0 * HALF, in1=lin[:, b, gs, :], op0=ALU.min, op1=ALU.mult
+                out=res[:, b, gs, :], in0=gate[:, b, gs, :], scalar=2.0 * HALF, in1=lin[:, b, gs, :],
+                op0=ALU.min, op1=ALU.mult,
             )
 
-        def clamp(b):
+        def clamp(b, gs):
             nc.vector.tensor_scalar(
-                out=gate[:, b, :, :], in0=lin[:, b, :, :], scalar1=-HALF, scalar2=HALF, op0=ALU.max, op1=ALU.min
+                out=gate[:, b, gs, :], in0=lin[:, b, gs, :], scalar1=-HALF, scalar2=HALF, op0=ALU.max, op1=ALU.min
             )
 
-        def finish_clamp(dst, b):
+        def finish_clamp(b, gs):
             nc.vector.scalar_tensor_tensor(
-                out=dst, in0=gate[:, b, :, :], scalar=HALF, in1=lin[:, b, :, :], op0=ALU.add, op1=ALU.mult
+                out=res[:, b, gs, :], in0=gate[:, b, gs, :], scalar=HALF, in1=lin[:, b, gs, :],
+                op0=ALU.add, op1=ALU.mult,
             )
 
-        out_rows = out.rearrange("g m n -> m g n")
-        vcopy = nc.vector.tensor_copy
-        scopy = nc.scalar.copy
-
-        load_x(0)
-        load_w(0, w0)
-        load_w(1, w1)
-        load_w(2, w2)
-        load_x(1)
-        load_x(2)
+        def store(b, gs):
+            nc.sync.dma_start(out=out_rows[:, gs, b * BLK : (b + 1) * BLK], in_=res[:, b, gs, :])
 
         nc.vector.memset(norm_rows[:], 0.0)
-        for k, v in enumerate((cs, cb)):
-            nc.scalar.dma_start(
-                out=norm_rows[0:P:32, 64 * k : 64 * (k + 1)].rearrange("q (g i) -> q g i", g=G),
-                in_=v.rearrange("g (q i) o -> q g (i o)", i=32),
-            )
-        nc.scalar.activation(out=norm_scaled[:], in_=norm_rows[:], func=ACT.Copy, scale=INV_SQRT6)
-        nc.vector.transpose(norm[:], norm_scaled[:])
-        nc.vector.tensor_scalar(out=shifted[:], in0=norm[:, 64:P:32], scalar1=HALF, scalar2=None, op0=ALU.add)
-
-        cast_x(vcopy, 0, 256)
-        cast_x(scopy, 256, 384)
-        cast_w(scopy, 0)
-        quantise(x_codes, x_scales, x_bf, 256, 384)
-        quantise(x_codes, x_scales, x_bf, 0, 256)
-        cast_w(vcopy, 1)
-        quantise(w_codes, w_scales, w_bf, 0, M)
-        cast_w(scopy, 2)
-        quantise(w_codes, w_scales, w_bf, M, 2 * M)
-        multiply(0, 0)
-        multiply(1, 0)
-        multiply(2, 0)
-        multiply(0, 1)
-        multiply(1, 1)
-        quantise(w_codes, w_scales, w_bf, 2 * M, 3 * M)
-        multiply(0, 2)
+        load("w", 0, 128)
+        load_norm(0)
+        load_norm(1)
+        load("x", 0, 512)
+        load("w", 128, 256)
+        load("w", 256, 384)
+        load("x", 512, 640)
+        load("x", 640, 768)
+        nc.gpsimd.memset(one[:], 1.0)
+        nc.scalar.activation(out=half[:], in_=one[:], func=ACT.Copy, scale=HALF)
+        cast(nc.vector.tensor_copy, "w", 0, 128)
+        nc.vector.transpose(norm_cols[:], norm_rows[:])
+        nc.scalar.activation(out=norm[:], in_=norm_cols[:, 0:P:32], func=ACT.Copy, scale=INV_SQRT6)
+        quantise("w", 0, 128)
+        nc.scalar.activation(out=shifted[:], in_=norm_cols[:, 64:P:32], func=ACT.Identity, scale=INV_SQRT6, bias=half[:])
+        warm(18)
+        cast(nc.vector.tensor_copy, "x", 0, 128)
+        cast(nc.scalar.copy, "x", 128, 256)
+        cast(nc.vector.tensor_copy, "x", 256, 384)
+        quantise("x", 0, 128)
+        cast(nc.scalar.copy, "w", 128, 256)
+        multiply(0, 0, 1)
+        quantise("x", 128, 256)
+        multiply(0, 0, 0)
+        multiply(1, 0, 1)
+        quantise("x", 256, 384)
+        multiply(1, 0, 0)
+        cast(nc.vector.tensor_copy, "w", 256, 320)
+        cast(nc.scalar.copy, "w", 320, 384)
+        quantise("w", 128, 256)
+        quantise("w", 256, 384)
+        multiply(2, 0, 1)
+        cast(nc.vector.tensor_copy, "x", 512, 608)
+        multiply(2, 0, 0)
+        multiply(0, 1, 0)
+        multiply(0, 1, 1)
+        cast(nc.scalar.copy, "x", 384, 512)
+        multiply(0, 2, 0)
+        cast(nc.scalar.copy, "x", 608, 640)
+        multiply(0, 2, 1)
+        quantise("x", 384, 512)
+        multiply(1, 1, 1)
+        gate_scalar(0, 0)
+        multiply(1, 1, 0)
+        multiply(1, 2, 1)
+        quantise("x", 512, 640)
+        multiply(2, 1, 1)
+        lin_vector(0, 1)
+        cast(nc.vector.tensor_copy, "x", 640, 704)
         lin_scalar(0, 0)
-        lin_scalar(0, 1)
-        cast_x(vcopy, 384, 544)
-        cast_x(scopy, 544, 640)
-        clamp(0)
-        quantise(x_codes, x_scales, x_bf, 384, 640)
-        multiply(1, 2)
-        multiply(2, 1)
-        multiply(2, 2)
-        multiply(3, 0)
-        multiply(3, 1)
-        finish_clamp(res_a[:], 0)
-        nc.sync.dma_start(out=out_rows[:, :, 0:BLK], in_=res_a[:])
-        cast_x(scopy, 704, 768)
-        cast_x(vcopy, 640, 704)
-        lin_scalar(1, 0)
+        finish_relu(0, slice(0, 1))
+        multiply(1, 2, 0)
+        cast(nc.scalar.copy, "x", 704, 768)
         lin_scalar(1, 1)
-        lin_vector(2, 0)
-        quantise(x_codes, x_scales, x_bf, 640, 768)
-        multiply(3, 2)
+        clamp(0, slice(1, 2))
+        quantise("x", 640, 768)
+        lin_scalar(1, 0)
+        clamp(1, slice(1, 2))
+        gate_scalar(1, 0)
+        multiply(2, 1, 0)
+        multiply(2, 2, 1)
+        multiply(3, 0, 1)
+        multiply(2, 2, 0)
+        finish_clamp(0, slice(1, 2))
+        multiply(3, 1, 1)
+        store(0, slice(0, 1))
+        multiply(3, 0, 0)
+        store(0, slice(1, 2))
+        finish_relu(1, slice(0, 1))
+        lin_scalar(2, 0)
+        gate_scalar(2, 1)
+        multiply(3, 1, 0)
+        store(1, slice(0, 1))
         lin_scalar(2, 1)
-        clamp(1)
-        clamp(2)
-        finish_clamp(res_b[:, :, 0:BLK], 1)
-        finish_clamp(res_b[:, :, BLK : 2 * BLK], 2)
-        nc.sync.dma_start(out=out_rows[:, :, BLK : 3 * BLK], in_=res_b[:])
-        gate_scalar(3, 0)
-        lin_scalar(3, 0)
+        multiply(3, 2, 1)
+        finish_clamp(1, slice(1, 2))
+        multiply(3, 2, 0)
+        clamp(2, slice(0, 1))
+        finish_relu(2, slice(1, 2))
+        finish_clamp(2, slice(0, 1))
         gate_scalar(3, 1)
-        lin_vector(3, 1)
-        finish_relu(res_c[:, 0:1, :], 3, slice(0, 1))
-        finish_relu(res_c[:, 1:2, :], 3, slice(1, 2))
-        nc.sync.dma_start(out=out_rows[:, :, 3 * BLK : 4 * BLK], in_=res_c[:])
+        lin_scalar(3, 1)
+        lin_scalar(3, 0)
+        store(1, slice(1, 2))
+        store(2, slice(1, 2))
+        gate_scalar(3, 0)
+        store(2, slice(0, 1))
+        finish_relu(3, slice(1, 2))
+        finish_relu(3, slice(0, 1))
+        store(3, slice(1, 2))
+        store(3, slice(0, 1))

import math
from contextlib import ExitStack

import concourse.mybir as mybir

G, D, M, N, L = 2, 256, 128, 512, 768
TAPS = 3
FLOPS = 2 * G * TAPS * D * M * N

F32 = mybir.dt.float32
BF16 = mybir.dt.bfloat16
U32 = mybir.dt.uint32
U8 = mybir.dt.uint8
FP8X4 = mybir.dt.float8_e4m3fn_x4
ACT = mybir.ActivationFunctionType
ALU = mybir.AluOpType

P = 128
PACK = 4
ROWS = D // PACK
BLK = 128
INV_SQRT6 = 1.0 / math.sqrt(6.0)
HALF = 3.0 * INV_SQRT6


def tile_rows_conv_bnhs_kernel(tc, x, w0, w1, w2, cs, cb, out):
    nc = tc.nc
    with ExitStack() as ctx:
        sb = ctx.enter_context(tc.tile_pool(name="sb", bufs=1))
        ps = ctx.enter_context(tc.psum_pool(name="ps", bufs=1))
        ctx.enter_context(tc.manual_schedule())

        src = {"x": x.rearrange("g (p j) l -> (g p) j l", j=PACK)}
        w_src = [w.rearrange("g (p j) m -> (g p) j m", j=PACK) for w in (w0, w1, w2)]
        width = {"x": L, "w": TAPS * M}
        pieces = [("w", 0, 128), ("x", 0, 512), ("w", 128, 256), ("w", 256, 384), ("x", 512, 640), ("x", 640, 768)]
        raw = {pc: sb.tile([P, PACK, pc[2] - pc[1]], F32, name="raw_%s%d" % pc[:2], align_bytes=64) for pc in pieces}
        bf = {n: sb.tile([P, width[n], PACK], BF16, name="bf_" + n, align_bytes=64) for n in width}
        codes = {n: sb.tile([P, width[n]], U32, name="codes_" + n, align_bytes=64) for n in width}
        scales = {n: sb.tile([P, width[n]], U8, name="scales_" + n, align_bytes=64) for n in width}
        norm_rows = sb.tile([P, P], F32, name="norm_rows", align_bytes=64)
        norm_cols = sb.tile([P, P], F32, name="norm_cols", align_bytes=64)
        norm = sb.tile([P, 2 * G], F32, name="norm", align_bytes=64)
        shifted = sb.tile([P, G], F32, name="shifted", align_bytes=64)
        one = sb.tile([P, 1], F32, name="one", align_bytes=64)
        half = sb.tile([P, 1], F32, name="half", align_bytes=64)
        acc = [[ps.tile([M, BLK], F32, name="acc%d_%d" % (g, b)) for b in range(N // BLK - g)] for g in range(G)]
        acc[1].append(acc[1][0])
        spare = ps.tile([M, BLK], F32, name="spare")
        lin = sb.tile([P, N // BLK, G, BLK], F32, name="lin", align_bytes=64)
        gate = sb.tile([P, N // BLK, G, BLK], F32, name="gate", align_bytes=64)
        res = sb.tile([P, N // BLK, G, BLK], F32, name="res", align_bytes=64)
        out_rows = out.rearrange("g m n -> m g n")

        def load(n, a, b):
            nc.sync.dma_start(out=raw[(n, a, b)][:], in_=src["x"][:, :, a:b] if n == "x" else w_src[a // M])

        def load_norm(k):
            nc.sync.dma_start(
                out=norm_rows[0:P:32, 64 * k : 64 * (k + 1)].rearrange("q (g i) -> q g i", g=G),
                in_=(cs, cb)[k].rearrange("g (q i) o -> q g (i o)", i=32),
            )

        def cast(copy, n, a, b):
            pc = [k for k in pieces if k[0] == n and k[1] <= a and b <= k[2]][0]
            copy(
                out=bf[n][:, a:b, :].rearrange("p (c i) j -> p c j i", i=4),
                in_=raw[pc][:, :, a - pc[1] : b - pc[1]].rearrange("p j (c i) -> p c j i", i=4),
            )

        def quantise(n, a, b):
            nc.vector.quantize_mx(
                out=codes[n][:, a:b].bitcast(FP8X4),
                scales=scales[n][:, a:b],
                in_=bf[n][:, a:b, :].rearrange("p c j -> p (c j)"),
            )

        def pass_mx(dst, g, wc, xc, start, stop):
            rows = slice(ROWS * g, ROWS * (g + 1))
            nc.tensor.matmul_mx(
                out=dst,
                lhsT=codes["w"][rows, wc].bitcast(FP8X4),
                lhsT_scale=scales["w"][rows, wc],
                rhs=codes["x"][rows, xc].bitcast(FP8X4),
                rhs_scale=scales["x"][rows, xc],
                start=start,
                stop=stop,
            )

        def multiply(b, t, g):
            pass_mx(
                acc[g][b][:, 0:BLK], g, slice(t * M, (t + 1) * M), slice((b + t) * BLK, (b + t + 1) * BLK),
                t == 0, t == TAPS - 1,
            )

        def warm(n):
            for i in range(n):
                nc.tensor.matmul_mx(
                    out=spare[:],
                    lhsT=codes["w"][:, 0:M].bitcast(FP8X4),
                    lhsT_scale=scales["w"][:, 0:M],
                    rhs=codes["w"][:, 0:M].bitcast(FP8X4),
                    rhs_scale=scales["w"][:, 0:M],
                    start=True,
                    stop=True,
                )

        def lin_scalar(b, g):
            nc.scalar.activation(
                out=lin[:, b, g, :], in_=acc[g][b][:, 0:BLK], func=ACT.Identity,
                scale=norm[:, g : g + 1], bias=norm[:, G + g : G + g + 1],
            )

        def lin_vector(b, g):
            nc.vector.tensor_scalar(
                out=lin[:, b, g, :], in0=acc[g][b][:, 0:BLK], scalar1=norm[:, g : g + 1],
                scalar2=norm[:, G + g : G + g + 1], op0=ALU.mult, op1=ALU.add,
            )

        def gate_scalar(b, g):
            nc.scalar.activation(
                out=gate[:, b, g, :], in_=acc[g][b][:, 0:BLK], func=ACT.Relu,
                scale=norm[:, g : g + 1], bias=shifted[:, g : g + 1],
            )

        def finish_relu(b, gs):
            nc.vector.scalar_tensor_tensor(
                out=res[:, b, gs, :], in0=gate[:, b, gs, :], scalar=2.0 * HALF, in1=lin[:, b, gs, :],
                op0=ALU.min, op1=ALU.mult,
            )

        def clamp(b, gs):
            nc.vector.tensor_scalar(
                out=gate[:, b, gs, :], in0=lin[:, b, gs, :], scalar1=-HALF, scalar2=HALF, op0=ALU.max, op1=ALU.min
            )

        def finish_clamp(b, gs):
            nc.vector.scalar_tensor_tensor(
                out=res[:, b, gs, :], in0=gate[:, b, gs, :], scalar=HALF, in1=lin[:, b, gs, :],
                op0=ALU.add, op1=ALU.mult,
            )

        def store(b, gs):
            nc.sync.dma_start(out=out_rows[:, gs, b * BLK : (b + 1) * BLK], in_=res[:, b, gs, :])

        nc.vector.memset(norm_rows[:], 0.0)
        load("w", 0, 128)
        load_norm(0)
        load_norm(1)
        load("x", 0, 512)
        load("w", 128, 256)
        load("w", 256, 384)
        load("x", 512, 640)
        load("x", 640, 768)
        nc.gpsimd.memset(one[:], 1.0)
        nc.scalar.activation(out=half[:], in_=one[:], func=ACT.Copy, scale=HALF)
        cast(nc.vector.tensor_copy, "w", 0, 128)
        nc.vector.transpose(norm_cols[:], norm_rows[:])
        nc.scalar.activation(out=norm[:], in_=norm_cols[:, 0:P:32], func=ACT.Copy, scale=INV_SQRT6)
        quantise("w", 0, 128)
        nc.scalar.activation(out=shifted[:], in_=norm_cols[:, 64:P:32], func=ACT.Identity, scale=INV_SQRT6, bias=half[:])
        warm(18)
        cast(nc.vector.tensor_copy, "x", 0, 128)
        cast(nc.scalar.copy, "x", 128, 256)
        cast(nc.vector.tensor_copy, "x", 256, 384)
        quantise("x", 0, 128)
        cast(nc.scalar.copy, "w", 128, 256)
        multiply(0, 0, 1)
        quantise("x", 128, 256)
        multiply(0, 0, 0)
        multiply(1, 0, 1)
        quantise("x", 256, 384)
        multiply(1, 0, 0)
        cast(nc.vector.tensor_copy, "w", 256, 320)
        cast(nc.scalar.copy, "w", 320, 384)
        quantise("w", 128, 256)
        quantise("w", 256, 384)
        multiply(2, 0, 1)
        cast(nc.vector.tensor_copy, "x", 512, 608)
        multiply(2, 0, 0)
        multiply(0, 1, 0)
        multiply(0, 1, 1)
        cast(nc.scalar.copy, "x", 384, 512)
        multiply(0, 2, 0)
        cast(nc.scalar.copy, "x", 608, 640)
        multiply(0, 2, 1)
        quantise("x", 384, 512)
        multiply(1, 1, 1)
        gate_scalar(0, 0)
        multiply(1, 1, 0)
        multiply(1, 2, 1)
        quantise("x", 512, 640)
        multiply(2, 1, 1)
        lin_vector(0, 1)
        cast(nc.vector.tensor_copy, "x", 640, 704)
        lin_scalar(0, 0)
        finish_relu(0, slice(0, 1))
        multiply(1, 2, 0)
        cast(nc.scalar.copy, "x", 704, 768)
        lin_scalar(1, 1)
        clamp(0, slice(1, 2))
        quantise("x", 640, 768)
        lin_scalar(1, 0)
        clamp(1, slice(1, 2))
        gate_scalar(1, 0)
        multiply(2, 1, 0)
        multiply(2, 2, 1)
        multiply(3, 0, 1)
        multiply(2, 2, 0)
        finish_clamp(0, slice(1, 2))
        multiply(3, 1, 1)
        store(0, slice(0, 1))
        multiply(3, 0, 0)
        store(0, slice(1, 2))
        finish_relu(1, slice(0, 1))
        lin_scalar(2, 0)
        gate_scalar(2, 1)
        multiply(3, 1, 0)
        store(1, slice(0, 1))
        lin_scalar(2, 1)
        multiply(3, 2, 1)
        finish_clamp(1, slice(1, 2))
        multiply(3, 2, 0)
        clamp(2, slice(0, 1))
        finish_relu(2, slice(1, 2))
        finish_clamp(2, slice(0, 1))
        gate_scalar(3, 1)
        lin_scalar(3, 1)
        lin_scalar(3, 0)
        store(1, slice(1, 2))
        store(2, slice(1, 2))
        gate_scalar(3, 0)
        store(2, slice(0, 1))
        finish_relu(3, slice(1, 2))
        finish_relu(3, slice(0, 1))
        store(3, slice(1, 2))
        store(3, slice(0, 1))
